import numpy as np, ml_dtypes
CORES = [33,38,57,62,81,86,161,166,185,190,209,214]
N = 12
import mx_ref
BF = ml_dtypes.bfloat16
def entries(a):
    return np.ascontiguousarray(a.T).reshape(-1)
def table(e):
    return np.ascontiguousarray(np.reshape(e, (-1, 16)).T).astype(np.int32)
def cols(t, e):
    v = np.concatenate([t.reshape(128, -1, 4), np.zeros((128, 1, 4), BF)], axis=1)
    return np.ascontiguousarray(v[:, e]).reshape(128, -1)
def f(rng, *shape):
    return mx_ref.flush((rng.standard_normal(shape, dtype=np.float32) * np.exp2(rng.integers(-2, 3, shape[:-1] + (1,)))).astype(BF))
def wide(rng, *shape, cols=0):
    v = rng.standard_normal(shape, dtype=np.float32) * np.exp2(rng.integers(-12, 13, shape)).astype(np.float32)
    if cols: v *= np.repeat(np.exp2(rng.integers(-cols, cols + 1, shape[:-2] + (1, shape[-1] // 4))) * (rng.random(shape[:-2] + (1, shape[-1] // 4)) > 0.0625), 4, axis=-1).astype(np.float32)
    return mx_ref.flush(v.astype(BF))
T, W, UN, CR = 512, 512, 160, 64
HOST = [0 if k < 128 else 1 for k in CORES]
def lists(rng, full=False, alike=False):
    uni, need, pos = np.full((N, 2, UN), -1), np.full((N, N, CR), -1), []
    for q in range(N):
        for g in range(2):
            mates = [r for r in range(N) if HOST[r] == g]
            n = UN if full else int(rng.integers(CR >> 1, CR + 1)) if alike else int(rng.integers(UN >> 2, UN + 1))
            at = rng.permutation(UN)[:n]
            uni[q, g, at] = rng.permutation(T)[:n]
            who = rng.permutation(np.repeat(np.arange(len(mates)), CR))[:n]
            for i, r in enumerate(mates):
                e, others = at[who == i], at[who != i]
                if alike: e = at
                else:
                    k = CR if full else int(rng.integers(max(len(e), CR >> 2), min(CR, n) + 1))
                    e = np.concatenate([e, rng.permutation(others)[:k - len(e)]])
                need[r, q, rng.permutation(CR)[:len(e)]] = e
    for r in range(N):
        ok = np.flatnonzero(need[r].reshape(-1) >= 0)
        pos.append(table(rng.permutation(ok)[:W] if full else rng.choice(ok, W)))
    return {"uni": np.stack([table(e.reshape(-1)) for e in uni]), "need": np.stack([table(e.reshape(-1)) for e in need]), "pos": np.stack(pos)}
def setup_inputs(rng):
    return {"c": f(rng, N, 128, 4 * T), "w": f(rng, N, 128, 512), **lists(rng)}
def setup_inputs_alike(rng):
    return {**setup_inputs(rng), **lists(rng, alike=True)}
def setup_inputs_pairs(rng):
    d = setup_inputs(rng)
    uni, need = np.full((N, 2, UN), -1), np.full((N, N, CR), -1)
    for g in range(2):
        mates = rng.permutation([r for r in range(N) if HOST[r] == g])
        for q in range(N):
            at = rng.permutation(UN)[:2 * CR]
            uni[q, g, at] = rng.permutation(T)[:2 * CR]
            for i, r in enumerate(mates):
                need[r, q] = rng.permutation(at[:CR] if i < len(mates) // 2 else at[CR:])
    pos = [table(rng.choice(N * CR, W)) for r in range(N)]
    return {**d, "uni": np.stack([table(e.reshape(-1)) for e in uni]), "need": np.stack([table(e.reshape(-1)) for e in need]), "pos": np.stack(pos)}
def setup_inputs_full(rng):
    return {**setup_inputs(rng), **lists(rng, full=True)}
def setup_inputs_few(rng):
    d = {**setup_inputs(rng), **lists(rng, full=True)}
    uni = np.stack([entries(e) for e in d["uni"]]).reshape(N, 2, UN)
    need = np.stack([entries(e) for e in d["need"]]).reshape(N, N, CR)
    pos = [None] * N
    for g in range(2):
        p = rng.permutation(N)
        h = [HOST[q] for q in p]
        lead = [h.index(0), h.index(1)]
        own = np.concatenate([p[lead], np.delete(p, lead)])[:-(-W // CR)]
        rest = np.setdiff1d(np.arange(N), own)
        uni[rest, g] = -1
        for r in range(N):
            if HOST[r] != g: continue
            need[r, rest] = -1
            s = rng.permutation(own)[:, None] * CR + np.arange(CR)
            s[-1] = rng.permutation(s[-1])
            pos[r] = table(rng.permutation(s.reshape(-1)[:W]))
    return {**d, "uni": np.stack([table(e.reshape(-1)) for e in uni]), "need": np.stack([table(e.reshape(-1)) for e in need]), "pos": np.stack(pos)}
def setup_inputs_spread(rng):
    d = setup_inputs(rng); d["c"] = wide(rng, N, 128, 4 * T, cols=6); return d
def check_inputs(d):
    b = []
    uni = np.stack([entries(e) for e in d["uni"]]).reshape(N, 2, UN)
    need = np.stack([entries(e) for e in d["need"]]).reshape(N, N, CR)
    if uni.min() < -1 or uni.max() >= T: b.append("uni")
    if need.min() < -1 or need.max() >= UN: return b + ["need"]
    for q in range(N):
        for g in range(2):
            e = uni[q, g][uni[q, g] >= 0]
            if len(set(e.tolist())) != len(e): b.append("a column of one owner twice for one host")
            named = set()
            for r in range(N):
                if HOST[r] != g: continue
                k = need[r, q][need[r, q] >= 0]
                if len(set(k.tolist())) != len(k): b.append("need names an entry of one union twice")
                if (uni[q, g][k] < 0).any(): b.append("need names an empty entry of uni")
                named |= set(k.tolist())
            if set(np.flatnonzero(uni[q, g] >= 0).tolist()) - named: b.append("an entry of uni that no rank of the host needs")
    for r in range(N):
        p = entries(d["pos"][r])
        if p.min() < 0 or p.max() >= N * CR or (need[r].reshape(-1)[p] < 0).any(): b.append("pos")
    return b
def reference(c, w, uni, need, pos):
    uni = np.stack([entries(e) for e in uni]).reshape(N, 2, UN)
    need = np.stack([entries(e) for e in need]).reshape(N, N, CR)
    y = np.zeros((N, 128, W), np.float32)
    for r in range(N):
        g = HOST[r]
        t = np.concatenate([cols(c[q], np.where(need[r, q] >= 0, uni[q, g][need[r, q]], -1)) for q in range(N)], axis=1)
        y[r] = mx_ref.matmul(mx_ref.quantize(w[r]), mx_ref.quantize(cols(t, entries(pos[r]))))
    return {"y": y}

@@ -1,0 +1,281 @@
+from concourse.bass import DstId, RemoteDMATransfer
+from concourse.mybir import dt, AluOpType, ActivationFunctionType
+
+UN, CR, W, CT = 160, 64, 512, 512
+BK = 2 * CR
+COPY = ActivationFunctionType.Copy
+CODE, PLANE = "float8_e4m3fn_x4", "uint8"
+SCRATCH = {
+    "cin": ("sbuf", [128, 4 * CT], "bfloat16"), "win": ("sbuf", [128, 512], "bfloat16"),
+    "qc": ("sbuf", [128, CT], CODE), "sc": ("sbuf", [128, CT], PLANE),
+    "qw": ("sbuf", [128, 128], CODE), "sw": ("sbuf", [128, 128], PLANE),
+    "nd": ("sbuf", [128, 12, 4], "int32"), "lsx": ("sbuf", [128, 6, 8], "uint16"),
+    "uni32": ("sbuf", [128, 20], "int32"), "uni16": ("sbuf", [128, 20], "uint16"),
+    "pos32": ("sbuf", [128, 32], "int32"), "pt": ("sbuf", [128, 32], "int32"), "pu": ("sbuf", [128, 32], "int32"),
+    "pv": ("sbuf", [128, 32], "int32"), "pw": ("sbuf", [128, 32], "int32"), "pos16": ("sbuf", [128, 32], "uint16"),
+    "uo": ("sbuf", [128, UN], CODE), "uos": ("sbuf", [128, UN], PLANE),
+    "uw": ("sbuf", [128, 2 * UN], CODE), "uws": ("sbuf", [128, 2 * UN], PLANE),
+    "ll": ("sbuf", [128, 40], "uint16"),
+    "rli": ("sbuf", [128, 6, 8], "uint16"), "rlw": ("sbuf", [128, 8], "uint16"),
+    "sd": ("sbuf", [128, 5 * BK], CODE), "sds": ("sbuf", [128, 5 * BK], PLANE),
+    "rl": ("sbuf", [128, 2 * BK], CODE), "rls": ("sbuf", [128, 2 * BK], PLANE),
+    "land": ("sbuf", [128, 6 * BK], CODE), "lands": ("sbuf", [128, 6 * BK], PLANE),
+    "ys": ("sbuf", [128, 6 * BK], "float32"), "yo": ("sbuf", [128, W], "float32"),
+    "acc": ("psum", [128, 512 * 6], "float32"),
+}
+SEMAPHORES = (["ldn", "ldu", "ldp", "ldw", "ldc0", "ldc1", "vnd", "vun", "vps", "vq", "vw", "vuo", "suo", "vuh", "suh",
+               "vown", "sown", "auc", "aus", "evv", "evs", "gv", "gs", "st0", "sent", "rlwa", "rlc", "rlp"]
+              + ["al%d" % i for i in range(3)] + ["vsd%d" % i for i in range(3)] + ["ssd%d" % i for i in range(3)]
+              + ["ap%d" % i for i in range(6)] + ["tm%d" % i for i in range(6)])
+
+
+def layout(T, topo):
+    pairs = []
+    for c in T.cores:
+        if not pairs or c not in topo.cores_of(pairs[-1][0]):
+            pairs.append([])
+        pairs[-1].append(c)
+    byhost = {}
+    for p, m in enumerate(pairs):
+        byhost.setdefault(topo.host(m[0]), []).append(p)
+    hub = []
+    for m in pairs:
+        mine = [d for d in T.cores if topo.host(d) == topo.host(m[0])]
+        hub.append([c for c in m if all(d == c or topo.may_write(c, d) for d in mine)][0])
+    return pairs, byhost, hub
+
+
+def rank_program(g, core, T, topo):
+    pairs, byhost, hub = layout(T, topo)
+    sem = T.sem
+    here = byhost.get(topo.host(core), [])
+    local = [c for p in here for c in pairs[p]]
+
+    def pair_of(c):
+        return [p for p, m in enumerate(pairs) if c in m][0]
+
+    def mate_of(c):
+        return [d for d in pairs[pair_of(c)] if d != c][0]
+
+    def direct(c, p):
+        return all(topo.may_write(c, d) for d in pairs[p])
+
+    def turn(p):
+        n = here.index(p)
+        return [here[(n + 1) % 3], here[(n + 2) % 3]]
+
+    def order_of(c):
+        o = turn(pair_of(c))
+        far_off = [not all(direct(d, pair_of(c)) for d in pairs[i]) for i in o]
+        return o[::-1] if far_off[1] and not far_off[0] else o
+
+    def blocked(c):
+        return [o for o in order_of(c) if not direct(c, o)]
+
+    def helper(c, p):
+        can = [h for h in topo.cores_of(c) if h not in T.cores and topo.die(h) == topo.die(c) and direct(h, p)]
+        return can[blocked(c).index(p)]
+
+    def on_off(c, other):
+        off = topo.engines(c, [d for d in T.cores if topo.host(d) != topo.host(c) and topo.may_write(c, d)][0])
+        return off, [e for e in topo.engines(c, other) if e not in off]
+
+    def hop(c, o):
+        off, on = on_off(c, helper(c, o))
+        if len(blocked(c)) == 1:
+            return off + on
+        return off if o == blocked(c)[0] else on
+
+    def dst(d):
+        rid, pid = topo.addr(d, core)
+        return DstId(rid=rid, pnc=pid)
+
+    def peers(c):
+        a, b = order_of(c)
+        return pairs[a] + pairs[b] + [mate_of(c)]
+
+    def group(c, d):
+        return min(peers(c).index(d) // 2, 2)
+
+    sent = [0]
+
+    def fused(transfers):
+        ts = []
+        for es, src, d, view, s in transfers:
+            ts.append(RemoteDMATransfer(dst_ids=[dst(d)], dma_engine_mask=sum(1 << e for e in es), remote_sem=sem[s],
+                                        srcs=[src], dsts=[view], alu_op=0))
+            sent[0] += len(es)
+        g.remote_dma_fused(ts, local_sem=sem.sent)
+
+    def u8(v):
+        return v.bitcast(dt.uint8)
+
+    def same(v):
+        return v
+
+    def put_list(es, src, c, d):
+        j = peers(d).index(c)
+        return (es, src[:, local.index(d), :], d, T.ll[:, 8 * j:8 * j + 8], "al%d" % group(d, c))
+
+    rank = T.rank_of(core)
+    if rank is None:
+        jobs = [(c, o) for c in local for o in turn(pair_of(c)) if not direct(c, o) and helper(c, o) == core]
+        if not jobs:
+            return
+        (c, o), = jobs
+        far = topo.engines(core, pairs[o][0])
+        h = len(far) // 2
+        n = 8 // len(blocked(c))
+        j = 8 * peers(c).index(mate_of(c)) + blocked(c).index(o) * n
+        g.wait_ge(sem.rlwa, 4)
+        fused([(far, T.rlw[:, 0:n], c, T.ll[:, j:j + n], "al2")])
+        a = local.index(c) * BK
+        for s, buf, lnd, cast in (("rlc", T.rl, T.land, u8), ("rlp", T.rls, T.lands, same)):
+            g.wait_ge(sem[s], len(hop(c, o)))
+            fused([(far[i * h:i * h + h], cast(buf[:, i * BK:(i + 1) * BK]), d, cast(lnd[:, a:a + BK]), "ap%d" % local.index(c))
+                   for i, d in enumerate(pairs[o])])
+        g.wait_ge(sem.sent, sent[0])
+        return
+
+    p = pair_of(core)
+    x = here.index(p)
+    away = [o for hh in byhost for o in byhost[hh] if o not in here]
+    mate = mate_of(core)
+    me = local.index(core)
+    order = order_of(core)
+    mine = peers(core)
+    partner = pairs[away[x]][pairs[p].index(core)]
+    far, near = on_off(core, mate)
+    h = len(far) // 2
+    hb, ab = T.rank_of(local[0]), T.rank_of(pairs[away[0]][0])
+    V, S, X = g.vector, g.scalar, g.tensor
+
+    def load(q, buf, src, s, groups):
+        for i in groups:
+            q.dma_start(buf[16 * i:16 * i + 16], src[:, :]).then_inc(sem[s], 16)
+
+    load(g.sync, T.nd, T.need, "ldn", range(0, 4))
+    load(S, T.nd, T.need, "ldn", range(4, 8))
+    for i in range(2):
+        S.dma_start(T.cin[:, 1024 * i:1024 * i + 1024], T.c[:, 1024 * i:1024 * i + 1024]).then_inc(sem["ldc%d" % i], 16)
+    load(g.sync, T.uni32, T.uni, "ldu", range(0, 8))
+    g.sync.wait_ge(sem.ldc0, 16)
+    g.sync.dma_start(T.win[:, :], T.w[:, :]).then_inc(sem.ldw, 16)
+    load(g.sync, T.pos32, T.pos, "ldp", range(0, 8))
+
+    V.wait_ge(sem.ldn, 128)
+    V.tensor_scalar(T.lsx[:, :, 0:4], T.nd[:, hb:hb + 6, :], UN, None, AluOpType.add).then_inc(sem.vnd, 1)
+    V.tensor_copy(T.lsx[:, :, 4:8], T.nd[:, ab:ab + 6, :]).then_inc(sem.vnd, 1)
+    g.wait_ge(sem.vnd, 2)
+    if blocked(core):
+        fused([(near, T.lsx[:, :, :], mate, T.rli[:, :, :], "al2")])
+    straight = [d for o in order if direct(core, o) for d in pairs[o]]
+    if straight:
+        fused([put_list(far[2 * i:2 * i + 2], T.lsx, core, d) for i, d in enumerate(straight)])
+    if blocked(mate):
+        n = 8 // len(blocked(mate))
+        fused([(near[4 * i:4 * i + 4], T.lsx[:, local.index(mate), n * i:n * i + n], helper(mate, o), T.rlw[:, 0:n], "rlwa")
+               for i, o in enumerate(blocked(mate))])
+        g.wait_ge(sem.al2, len(near))
+        to = [d for o in blocked(mate) for d in pairs[o]]
+        n = len(far) // len(to)
+        fused([put_list(far[n * i:n * i + n], T.rli, mate, d) for i, d in enumerate(to)])
+
+    def list_count(d):
+        if d == mate:
+            return len(near) if blocked(d) else len(far) * len(blocked(core))
+        return 2 if direct(d, p) else len(far) // (2 * len(blocked(d)))
+
+    for i in range(2):
+        a, b = 256 * i, 256 * i + 256
+        V.wait_ge(sem["ldc%d" % i], 16)
+        V.quantize_mx(T.qc[:, a:b], T.sc[:, a:b], T.cin[:, 4 * a:4 * b]).then_inc(sem.vq, 1)
+    V.wait_ge(sem.ldu, 128)
+    V.tensor_copy(T.uni16[:, :], T.uni32[:, :]).then_inc(sem.vun, 1)
+
+    def pick(codes, planes, c0, c1, wc, wp, n, off, vs, ss):
+        V.tensor_copy(codes[:, c0:c1].bitcast(dt.uint32), wc[:, 0:n].bitcast(dt.uint32).indirect(off)).then_inc(sem[vs], 1)
+        S.activation(planes[:, c0:c1], wp[:, 0:n].indirect(off), COPY).then_inc(sem[ss], 1)
+
+    for q in (V, S):
+        q.wait_ge(sem.vun, 1)
+        q.wait_ge(sem.vq, 2)
+    host = topo.host(core)
+    o10, h10 = 10 * (1 - host), 10 * host
+    pick(T.uo, T.uos, 0, UN, T.qc, T.sc, CT, T.uni16[:, o10:o10 + 10], "vuo", "suo")
+    pick(T.uw, T.uws, UN, 2 * UN, T.qc, T.sc, CT, T.uni16[:, h10:h10 + 10], "vuh", "suh")
+    g.wait_ge(sem.vuo, 1)
+    fused([(far, u8(T.uo[:, :]), partner, u8(T.uw[:, 0:UN]), "auc")])
+    g.wait_ge(sem.suo, 1)
+    fused([(far, T.uos[:, :], partner, T.uws[:, 0:UN], "aus")])
+
+    V.wait_ge(sem.ldw, 16)
+    V.quantize_mx(T.qw[:, :], T.sw[:, :], T.win[:, :]).then_inc(sem.vw, 1)
+    own_c, away_c = -BK * hb, CR - BK * ab
+    low, high = (own_c, away_c) if hb < ab else (away_c, own_c)
+    V.wait_ge(sem.ldp, 128)
+    V.tensor_scalar(T.pt[:, :], T.pos32[:, :], -CR, None, AluOpType.bitwise_and).then_inc(sem.vps, 1)
+    V.wait_ge(sem.vps, 1)
+    V.tensor_tensor(T.pu[:, :], T.pos32[:, :], T.pt[:, :], AluOpType.add).then_inc(sem.vps, 1)
+    V.tensor_scalar(T.pv[:, :], T.pt[:, :], 6 * CR, high - low, AluOpType.is_ge, AluOpType.mult).then_inc(sem.vps, 1)
+    V.wait_ge(sem.vps, 3)
+    V.tensor_tensor(T.pw[:, :], T.pu[:, :], T.pv[:, :], AluOpType.add).then_inc(sem.vps, 1)
+    V.wait_ge(sem.vps, 4)
+    V.tensor_scalar(T.pos16[:, :], T.pw[:, :], low, None, AluOpType.add).then_inc(sem.vps, 1)
+
+    V.wait_ge(sem.vuh, 1)
+    S.wait_ge(sem.suh, 1)
+    S.wait_ge(sem.vnd, 2)
+    V.wait_ge(sem.vnd, 2)
+    V.wait_ge(sem.auc, len(far))
+    S.wait_ge(sem.aus, len(far))
+    a = me * BK
+    for i in range(2):
+        for q in (V, S):
+            q.wait_ge(sem["al%d" % i], list_count(mine[2 * i]) + list_count(mine[2 * i + 1]))
+        pick(T.sd, T.sds, 2 * i * BK, (2 * i + 2) * BK, T.uw, T.uws, 2 * UN, T.ll[:, 16 * i:16 * i + 16], "vsd%d" % i, "ssd%d" % i)
+        for vs, buf, lnd, relay, rsem, cast in (("vsd%d" % i, T.sd, T.land, T.rl, "rlc", u8), ("ssd%d" % i, T.sds, T.lands, T.rls, "rlp", same)):
+            g.wait_ge(sem[vs], 1)
+            if direct(core, order[i]):
+                fused([(far[m * h:m * h + h], cast(buf[:, (2 * i + m) * BK:(2 * i + m + 1) * BK]), d, cast(lnd[:, a:a + BK]), "ap%d" % me)
+                       for m, d in enumerate(pairs[order[i]])])
+            else:
+                fused([(hop(core, order[i]), cast(buf[:, 2 * i * BK:(2 * i + 2) * BK]), helper(core, order[i]), cast(relay[:, :]), rsem)])
+    pick(T.land, T.lands, a, a + BK, T.uw, T.uws, 2 * UN, T.lsx[:, me, :], "vown", "sown")
+    for q in (V, S):
+        q.wait_ge(sem.al2, list_count(mate))
+    off = T.rli[:, me, :] if blocked(mate) else T.ll[:, 32:40]
+    pick(T.sd, T.sds, 4 * BK, 5 * BK, T.uw, T.uws, 2 * UN, off, "vsd2", "ssd2")
+    for vs, buf, lnd, cast in (("vsd2", T.sd, T.land, u8), ("ssd2", T.sds, T.lands, same)):
+        g.wait_ge(sem[vs], 1)
+        fused([(near, cast(buf[:, 4 * BK:5 * BK]), mate, cast(lnd[:, a:a + BK]), "ap%d" % me)])
+
+    seq = [core, mate] + [d for d in mine[:4] if direct(d, p)] + [d for d in mine[:4] if not direct(d, p)]
+    X.wait_ge(sem.vw, 1)
+    for i, d in enumerate(seq):
+        j = local.index(d)
+        if d == core:
+            X.wait_ge(sem.vown, 1)
+            X.wait_ge(sem.sown, 1)
+        else:
+            X.wait_ge(sem["ap%d" % j], 2 * len(near) if d == mate else 2 * h)
+        b = j * BK
+        X.matmul_mx(T.acc[:, 512 * i:512 * i + BK], T.qw[:, :], T.sw[:, :], T.land[:, b:b + BK], T.lands[:, b:b + BK], True, True).then_inc(sem["tm%d" % i], 1)
+        q = (S, V)[i % 2]
+        q.wait_ge(sem["tm%d" % i], 1)
+        if i % 2:
+            V.tensor_copy(T.ys[:, b:b + BK], T.acc[:, 512 * i:512 * i + BK]).then_inc(sem.evv, 1)
+        else:
+            S.activation(T.ys[:, b:b + BK], T.acc[:, 512 * i:512 * i + BK], COPY).then_inc(sem.evs, 1)
+
+    for q in (V, S):
+        q.wait_ge(sem.evv, 3)
+        q.wait_ge(sem.evs, 3)
+        q.wait_ge(sem.vps, 5)
+    V.tensor_copy(T.yo[:, 0:256], T.ys[:, :].indirect(T.pos16[:, 0:16])).then_inc(sem.gv, 1)
+    S.activation(T.yo[:, 256:512], T.ys[:, :].indirect(T.pos16[:, 16:32]), COPY).then_inc(sem.gs, 1)
+    g.sync.wait_ge(sem.gv, 1)
+    g.sync.wait_ge(sem.gs, 1)
+    g.sync.dma_start(T.y[:, :], T.yo[:, :]).then_inc(sem.st0, 16)
+    g.sync.wait_ge(sem.st0, 16)
+    g.wait_ge(sem.sent, sent[0])

@@ -3,6 +3,8 @@ from concourse.mybir import dt, AluOpType, ActivationFunctionType
 
 UN, CR, W, CT = 160, 64, 512, 512
 BK = 2 * CR
+C0 = 352
+Y0 = 192
 COPY = ActivationFunctionType.Copy
 CODE, PLANE = "float8_e4m3fn_x4", "uint8"
 SCRATCH = {
@@ -15,94 +17,91 @@ SCRATCH = {
     "pv": ("sbuf", [128, 32], "int32"), "pw": ("sbuf", [128, 32], "int32"), "pos16": ("sbuf", [128, 32], "uint16"),
     "uo": ("sbuf", [128, UN], CODE), "uos": ("sbuf", [128, UN], PLANE),
     "uw": ("sbuf", [128, 2 * UN], CODE), "uws": ("sbuf", [128, 2 * UN], PLANE),
-    "ll": ("sbuf", [128, 40], "uint16"),
-    "rli": ("sbuf", [128, 6, 8], "uint16"), "rlw": ("sbuf", [128, 8], "uint16"),
-    "sd": ("sbuf", [128, 5 * BK], CODE), "sds": ("sbuf", [128, 5 * BK], PLANE),
+    "ll": ("sbuf", [128, 6, 8], "uint16"),
+    "rli": ("sbuf", [128, 2, 8], "uint16"),
+    "sd": ("sbuf", [128, 6 * BK], CODE), "sds": ("sbuf", [128, 6 * BK], PLANE),
     "rl": ("sbuf", [128, 2 * BK], CODE), "rls": ("sbuf", [128, 2 * BK], PLANE),
     "land": ("sbuf", [128, 6 * BK], CODE), "lands": ("sbuf", [128, 6 * BK], PLANE),
     "ys": ("sbuf", [128, 6 * BK], "float32"), "yo": ("sbuf", [128, W], "float32"),
     "acc": ("psum", [128, 512 * 6], "float32"),
 }
 SEMAPHORES = (["ldn", "ldu", "ldp", "ldw", "ldc0", "ldc1", "vnd", "vun", "vps", "vq", "vw", "vuo", "suo", "vuh", "suh",
-               "vown", "sown", "auc", "aus", "evv", "evs", "gv", "gs", "st0", "sent", "rlwa", "rlc", "rlp"]
-              + ["al%d" % i for i in range(3)] + ["vsd%d" % i for i in range(3)] + ["ssd%d" % i for i in range(3)]
-              + ["ap%d" % i for i in range(6)] + ["tm%d" % i for i in range(6)])
-
-
-def layout(T, topo):
-    pairs = []
-    for c in T.cores:
-        if not pairs or c not in topo.cores_of(pairs[-1][0]):
-            pairs.append([])
-        pairs[-1].append(c)
-    byhost = {}
-    for p, m in enumerate(pairs):
-        byhost.setdefault(topo.host(m[0]), []).append(p)
-    hub = []
-    for m in pairs:
-        mine = [d for d in T.cores if topo.host(d) == topo.host(m[0])]
-        hub.append([c for c in m if all(d == c or topo.may_write(c, d) for d in mine)][0])
-    return pairs, byhost, hub
+               "vown", "sown", "auc", "aus", "evv", "evs", "gv", "gs", "st0", "sent", "rla", "rc0", "rc1", "rp0", "rp1"]
+              + ["vsd%d" % i for i in range(3)] + ["ssd%d" % i for i in range(3)]
+              + ["al%d" % i for i in range(6)] + ["ap%d" % i for i in range(6)] + ["tm%d" % i for i in range(6)])
 
 
 def rank_program(g, core, T, topo):
-    pairs, byhost, hub = layout(T, topo)
     sem = T.sem
-    here = byhost.get(topo.host(core), [])
-    local = [c for p in here for c in pairs[p]]
-
-    def pair_of(c):
-        return [p for p, m in enumerate(pairs) if c in m][0]
+    local = [c for c in T.cores if topo.host(c) == topo.host(core)]
+    away = [c for c in T.cores if c not in local]
 
     def mate_of(c):
-        return [d for d in pairs[pair_of(c)] if d != c][0]
+        return [d for d in local if d != c and d in topo.cores_of(c)][0]
 
-    def direct(c, p):
-        return all(topo.may_write(c, d) for d in pairs[p])
-
-    def turn(p):
-        n = here.index(p)
-        return [here[(n + 1) % 3], here[(n + 2) % 3]]
-
-    def order_of(c):
-        o = turn(pair_of(c))
-        far_off = [not all(direct(d, pair_of(c)) for d in pairs[i]) for i in o]
-        return o[::-1] if far_off[1] and not far_off[0] else o
+    def others(c):
+        n = local.index(c)
+        return [d for d in local[n + 1:] + local[:n] if d != mate_of(c)]
 
     def blocked(c):
-        return [o for o in order_of(c) if not direct(c, o)]
+        return [d for d in others(c) if not topo.may_write(c, d)]
 
-    def helper(c, p):
-        can = [h for h in topo.cores_of(c) if h not in T.cores and topo.die(h) == topo.die(c) and direct(h, p)]
-        return can[blocked(c).index(p)]
+    def handed(c):
+        if blocked(c):
+            return blocked(c)
+        can = [d for d in others(c) if topo.may_write(d, c)]
+        return ([d for d in can if blocked(d)] + can)[:1]
 
-    def on_off(c, other):
+    def helper(c, d):
+        to = handed(c)
+        can = [h for h in topo.cores_of(c) if h not in T.cores and topo.die(h) == topo.die(c) and all(topo.may_write(h, e) for e in to)]
+        return can[to.index(d) // 2]
+
+    def by_mate(c):
+        return [d for d in blocked(c) if c in blocked(d)]
+
+    def late(c, d):
+        return 0 if c not in handed(d) else 1 if c in by_mate(d) else 2
+
+    def on_off(c):
         off = topo.engines(c, [d for d in T.cores if topo.host(d) != topo.host(c) and topo.may_write(c, d)][0])
-        return off, [e for e in topo.engines(c, other) if e not in off]
+        return off, [e for e in topo.engines(c, mate_of(c)) if e not in off]
 
-    def hop(c, o):
-        off, on = on_off(c, helper(c, o))
-        if len(blocked(c)) == 1:
-            return off + on
-        return off if o == blocked(c)[0] else on
+    def stages(c):
+        far, near = on_off(c)
+        via = sorted(handed(c), key=lambda d: late(c, d))
+        straight = sorted([d for d in others(c) if d not in via], key=lambda d: late(c, d))
+        if len(via) == 1:
+            return [[(far, straight[0]), (near, via[0])], [(far[:4], straight[1]), (far[4:], straight[2]), (near, mate_of(c))]]
+        first = straight or via[0::2]
+        second = via if straight else via[1::2]
+        return [[(far, first[0]), (near, second[0])], [(far, first[1]), (near, second[1])], [(far + near, mate_of(c))]]
 
-    def dst(d):
-        rid, pid = topo.addr(d, core)
-        return DstId(rid=rid, pnc=pid)
+    def served(c, h):
+        return [d for st in stages(c) for _, d in st if d in handed(c) and helper(c, d) == h]
 
-    def peers(c):
-        a, b = order_of(c)
-        return pairs[a] + pairs[b] + [mate_of(c)]
+    def place(c, d):
+        return [(i, es) for i, st in enumerate(stages(c)) for es, e in st if e == d][0]
 
-    def group(c, d):
-        return min(peers(c).index(d) // 2, 2)
+    def list_calls(c):
+        far, near = on_off(c)
+        via = handed(c)
+        straight = [d for d in others(c) if d not in via]
+        on = near if straight else far + near
+        n = len(on) // len(via)
+        first = [(on[n * i:n * i + n], d) for i, d in enumerate(via)] + [(far[4 * i:4 * i + 4], d) for i, d in enumerate(straight[:2])]
+        return [first, [(far, d) for d in straight[2:]] + [(near, mate_of(c))]]
+
+    def list_engines(c, d):
+        return [es for call in list_calls(c) for es, e in call if e == d][0]
 
     sent = [0]
 
     def fused(transfers):
         ts = []
         for es, src, d, view, s in transfers:
-            ts.append(RemoteDMATransfer(dst_ids=[dst(d)], dma_engine_mask=sum(1 << e for e in es), remote_sem=sem[s],
+            rid, pid = topo.addr(d, core)
+            ts.append(RemoteDMATransfer(dst_ids=[DstId(rid=rid, pnc=pid)], dma_engine_mask=sum(1 << e for e in es), remote_sem=sem[s],
                                         srcs=[src], dsts=[view], alu_op=0))
             sent[0] += len(es)
         g.remote_dma_fused(ts, local_sem=sem.sent)
@@ -113,152 +112,167 @@ def rank_program(g, core, T, topo):
     def same(v):
         return v
 
-    def put_list(es, src, c, d):
-        j = peers(d).index(c)
-        return (es, src[:, local.index(d), :], d, T.ll[:, 8 * j:8 * j + 8], "al%d" % group(d, c))
-
     rank = T.rank_of(core)
     if rank is None:
-        jobs = [(c, o) for c in local for o in turn(pair_of(c)) if not direct(c, o) and helper(c, o) == core]
+        jobs = [c for c in local if any(helper(c, d) == core for d in handed(c))]
         if not jobs:
             return
-        (c, o), = jobs
-        far = topo.engines(core, pairs[o][0])
-        h = len(far) // 2
-        n = 8 // len(blocked(c))
-        j = 8 * peers(c).index(mate_of(c)) + blocked(c).index(o) * n
-        g.wait_ge(sem.rlwa, 4)
-        fused([(far, T.rlw[:, 0:n], c, T.ll[:, j:j + n], "al2")])
-        a = local.index(c) * BK
-        for s, buf, lnd, cast in (("rlc", T.rl, T.land, u8), ("rlp", T.rls, T.lands, same)):
-            g.wait_ge(sem[s], len(hop(c, o)))
-            fused([(far[i * h:i * h + h], cast(buf[:, i * BK:(i + 1) * BK]), d, cast(lnd[:, a:a + BK]), "ap%d" % local.index(c))
-                   for i, d in enumerate(pairs[o])])
+        c, = jobs
+        to = served(c, core)
+        far = topo.engines(core, to[0])
+        j = local.index(c)
+        d, = [e for e in to if e not in by_mate(c)]
+        g.wait_ge(sem.rla, len(list_engines(c, d)))
+        fused([(far, T.rli[:, 0, :], d, T.ll[:, j, :], "al%d" % j)])
+        for i, d in enumerate(to):
+            for s, buf, lnd, cast in (("rc", T.rl, T.land, u8), ("rp", T.rls, T.lands, same)):
+                g.wait_ge(sem[s + str(i)], len(place(c, d)[1]))
+                fused([(far, cast(buf[:, i * BK:(i + 1) * BK]), d, cast(lnd[:, j * BK:(j + 1) * BK]), "ap%d" % j)])
         g.wait_ge(sem.sent, sent[0])
         return
 
-    p = pair_of(core)
-    x = here.index(p)
-    away = [o for hh in byhost for o in byhost[hh] if o not in here]
     mate = mate_of(core)
     me = local.index(core)
-    order = order_of(core)
-    mine = peers(core)
-    partner = pairs[away[x]][pairs[p].index(core)]
-    far, near = on_off(core, mate)
-    h = len(far) // 2
-    hb, ab = T.rank_of(local[0]), T.rank_of(pairs[away[0]][0])
-    V, S, X = g.vector, g.scalar, g.tensor
+    partner = away[me]
+    far, near = on_off(core)
+    hb, ab = T.rank_of(local[0]), T.rank_of(away[0])
+    V, S, X, Y = g.vector, g.scalar, g.tensor, g.sync
+    halves = (slice(0, 64), slice(64, 128))
 
     def load(q, buf, src, s, groups):
         for i in groups:
             q.dma_start(buf[16 * i:16 * i + 16], src[:, :]).then_inc(sem[s], 16)
 
-    load(g.sync, T.nd, T.need, "ldn", range(0, 4))
-    load(S, T.nd, T.need, "ldn", range(4, 8))
-    for i in range(2):
-        S.dma_start(T.cin[:, 1024 * i:1024 * i + 1024], T.c[:, 1024 * i:1024 * i + 1024]).then_inc(sem["ldc%d" % i], 16)
-    load(g.sync, T.uni32, T.uni, "ldu", range(0, 8))
-    g.sync.wait_ge(sem.ldc0, 16)
-    g.sync.dma_start(T.win[:, :], T.w[:, :]).then_inc(sem.ldw, 16)
-    load(g.sync, T.pos32, T.pos, "ldp", range(0, 8))
+    load(Y, T.nd, T.need, "ldn", range(0, 2))
+    load(S, T.nd, T.need, "ldn", range(2, 4))
+    S.dma_start(T.cin[:, 0:4 * C0], T.c[:, 0:4 * C0]).then_inc(sem.ldc0, 16)
+    load(Y, T.uni32, T.uni, "ldu", range(0, 4))
+    Y.dma_start(T.cin[:, 4 * C0:], T.c[:, 4 * C0:]).then_inc(sem.ldc1, 16)
 
-    V.wait_ge(sem.ldn, 128)
-    V.tensor_scalar(T.lsx[:, :, 0:4], T.nd[:, hb:hb + 6, :], UN, None, AluOpType.add).then_inc(sem.vnd, 1)
-    V.tensor_copy(T.lsx[:, :, 4:8], T.nd[:, ab:ab + 6, :]).then_inc(sem.vnd, 1)
-    g.wait_ge(sem.vnd, 2)
-    if blocked(core):
-        fused([(near, T.lsx[:, :, :], mate, T.rli[:, :, :], "al2")])
-    straight = [d for o in order if direct(core, o) for d in pairs[o]]
-    if straight:
-        fused([put_list(far[2 * i:2 * i + 2], T.lsx, core, d) for i, d in enumerate(straight)])
-    if blocked(mate):
-        n = 8 // len(blocked(mate))
-        fused([(near[4 * i:4 * i + 4], T.lsx[:, local.index(mate), n * i:n * i + n], helper(mate, o), T.rlw[:, 0:n], "rlwa")
-               for i, o in enumerate(blocked(mate))])
-        g.wait_ge(sem.al2, len(near))
-        to = [d for o in blocked(mate) for d in pairs[o]]
-        n = len(far) // len(to)
-        fused([put_list(far[n * i:n * i + n], T.rli, mate, d) for i, d in enumerate(to)])
+    V.wait_ge(sem.ldn, 64)
+    for hf in halves:
+        V.tensor_copy(T.lsx[hf, :, 0:4], T.nd[0:64, hb:hb + 6, :]).then_inc(sem.vnd, 1)
+        V.tensor_scalar(T.lsx[hf, :, 4:8], T.nd[0:64, ab:ab + 6, :], UN, None, AluOpType.add).then_inc(sem.vnd, 1)
+    g.wait_ge(sem.vnd, 4)
+    for call in list_calls(core):
+        ts = []
+        for es, d in call:
+            src = T.lsx[:, local.index(d), :]
+            if d in by_mate(core):
+                ts.append((es, src, mate, T.rli[:, by_mate(core).index(d), :], "rla"))
+            elif d in handed(core):
+                ts.append((es, src, helper(core, d), T.rli[:, 0, :], "rla"))
+            else:
+                ts.append((es, src, d, T.ll[:, me, :], "al%d" % me))
+        fused(ts)
 
-    def list_count(d):
-        if d == mate:
-            return len(near) if blocked(d) else len(far) * len(blocked(core))
-        return 2 if direct(d, p) else len(far) // (2 * len(blocked(d)))
+    def wait_list(d):
+        n = (len(list_engines(d, core)), len(far) // max(1, len(by_mate(d))), len(far))[late(core, d)]
+        for q in (V, S):
+            q.wait_ge(sem["al%d" % local.index(d)], n)
 
-    for i in range(2):
-        a, b = 256 * i, 256 * i + 256
-        V.wait_ge(sem["ldc%d" % i], 16)
-        V.quantize_mx(T.qc[:, a:b], T.sc[:, a:b], T.cin[:, 4 * a:4 * b]).then_inc(sem.vq, 1)
-    V.wait_ge(sem.ldu, 128)
-    V.tensor_copy(T.uni16[:, :], T.uni32[:, :]).then_inc(sem.vun, 1)
+    V.wait_ge(sem.ldc0, 16)
+    V.quantize_mx(T.qc[:, 0:C0], T.sc[:, 0:C0], T.cin[:, 0:4 * C0]).then_inc(sem.vq, 1)
+    V.wait_ge(sem.ldu, 64)
+    for hf in halves:
+        V.tensor_copy(T.uni16[hf, :], T.uni32[0:64, :]).then_inc(sem.vun, 1)
+    V.wait_ge(sem.ldc1, 16)
+    V.quantize_mx(T.qc[:, C0:], T.sc[:, C0:], T.cin[:, 4 * C0:]).then_inc(sem.vq, 1)
 
     def pick(codes, planes, c0, c1, wc, wp, n, off, vs, ss):
         V.tensor_copy(codes[:, c0:c1].bitcast(dt.uint32), wc[:, 0:n].bitcast(dt.uint32).indirect(off)).then_inc(sem[vs], 1)
         S.activation(planes[:, c0:c1], wp[:, 0:n].indirect(off), COPY).then_inc(sem[ss], 1)
 
     for q in (V, S):
-        q.wait_ge(sem.vun, 1)
+        q.wait_ge(sem.vun, 2)
         q.wait_ge(sem.vq, 2)
     host = topo.host(core)
     o10, h10 = 10 * (1 - host), 10 * host
     pick(T.uo, T.uos, 0, UN, T.qc, T.sc, CT, T.uni16[:, o10:o10 + 10], "vuo", "suo")
-    pick(T.uw, T.uws, UN, 2 * UN, T.qc, T.sc, CT, T.uni16[:, h10:h10 + 10], "vuh", "suh")
+    pick(T.uw, T.uws, 0, UN, T.qc, T.sc, CT, T.uni16[:, h10:h10 + 10], "vuh", "suh")
     g.wait_ge(sem.vuo, 1)
-    fused([(far, u8(T.uo[:, :]), partner, u8(T.uw[:, 0:UN]), "auc")])
+    fused([(far, u8(T.uo[:, :]), partner, u8(T.uw[:, UN:]), "auc")])
     g.wait_ge(sem.suo, 1)
-    fused([(far, T.uos[:, :], partner, T.uws[:, 0:UN], "aus")])
+    fused([(far, T.uos[:, :], partner, T.uws[:, UN:], "aus")])
+    if by_mate(mate):
+        n, j = len(far) // len(by_mate(mate)), local.index(mate)
+        g.wait_ge(sem.rla, sum(len(list_engines(mate, d)) for d in by_mate(mate)))
+        fused([(far[n * i:n * i + n], T.rli[:, i, :], d, T.ll[:, j, :], "al%d" % j) for i, d in enumerate(by_mate(mate))])
+
+    plan = stages(core)
+    count = [0] * 3
+    V.wait_ge(sem.vuh, 1)
+    S.wait_ge(sem.suh, 1)
+    S.wait_ge(sem.vnd, 4)
+    V.wait_ge(sem.vnd, 4)
+    a = me * BK
+    pick(T.land, T.lands, a, a + CR, T.uw, T.uws, UN, T.lsx[:, me, 0:4], "vown", "sown")
+
+    Y.wait_ge(sem.vown, 1)
+    Y.dma_start(T.win[:, :], T.w[:, :]).then_inc(sem.ldw, 16)
+    load(Y, T.pos32, T.pos, "ldp", range(0, 4))
+
+    def part(i, d, lo, hi):
+        j = local.index(d)
+        pick(T.sd, T.sds, j * BK + lo, j * BK + hi, T.uw, T.uws, UN if hi == CR else 2 * UN, T.ll[:, j, lo // 16:hi // 16], "vsd%d" % i, "ssd%d" % i)
+        count[i] += 1
+
+    for i, st in enumerate(plan):
+        for _, d in st:
+            if not late(core, d):
+                wait_list(d)
+                part(i, d, 0, CR)
+    V.wait_ge(sem.auc, len(far))
+    S.wait_ge(sem.aus, len(far))
+    for i, st in enumerate(plan):
+        for _, d in sorted(st, key=lambda t: late(core, t[1])):
+            if late(core, d):
+                wait_list(d)
+            part(i, d, 0 if late(core, d) else CR, BK)
+        for k, vs, buf, lnd, relay, cast in (("rc", "vsd%d" % i, T.sd, T.land, T.rl, u8), ("rp", "ssd%d" % i, T.sds, T.lands, T.rls, same)):
+            g.wait_ge(sem[vs], count[i])
+            ts = []
+            for es, d in st:
+                j = local.index(d)
+                src = cast(buf[:, j * BK:(j + 1) * BK])
+                if d in handed(core):
+                    h = helper(core, d)
+                    n = served(core, h).index(d)
+                    ts.append((es, src, h, cast(relay[:, n * BK:(n + 1) * BK]), k + str(n)))
+                else:
+                    ts.append((es, src, d, cast(lnd[:, a:a + BK]), "ap%d" % me))
+            fused(ts)
+    pick(T.land, T.lands, a + CR, a + BK, T.uw, T.uws, 2 * UN, T.lsx[:, me, 4:8], "vown", "sown")
 
     V.wait_ge(sem.ldw, 16)
     V.quantize_mx(T.qw[:, :], T.sw[:, :], T.win[:, :]).then_inc(sem.vw, 1)
     own_c, away_c = -BK * hb, CR - BK * ab
     low, high = (own_c, away_c) if hb < ab else (away_c, own_c)
-    V.wait_ge(sem.ldp, 128)
-    V.tensor_scalar(T.pt[:, :], T.pos32[:, :], -CR, None, AluOpType.bitwise_and).then_inc(sem.vps, 1)
+    lo = halves[0]
+    V.wait_ge(sem.ldp, 64)
+    V.tensor_scalar(T.pt[lo, :], T.pos32[lo, :], -CR, None, AluOpType.bitwise_and).then_inc(sem.vps, 1)
     V.wait_ge(sem.vps, 1)
-    V.tensor_tensor(T.pu[:, :], T.pos32[:, :], T.pt[:, :], AluOpType.add).then_inc(sem.vps, 1)
-    V.tensor_scalar(T.pv[:, :], T.pt[:, :], 6 * CR, high - low, AluOpType.is_ge, AluOpType.mult).then_inc(sem.vps, 1)
+    V.tensor_tensor(T.pu[lo, :], T.pos32[lo, :], T.pt[lo, :], AluOpType.add).then_inc(sem.vps, 1)
+    V.tensor_scalar(T.pv[lo, :], T.pt[lo, :], 6 * CR, high - low, AluOpType.is_ge, AluOpType.mult).then_inc(sem.vps, 1)
     V.wait_ge(sem.vps, 3)
-    V.tensor_tensor(T.pw[:, :], T.pu[:, :], T.pv[:, :], AluOpType.add).then_inc(sem.vps, 1)
+    V.tensor_tensor(T.pw[lo, :], T.pu[lo, :], T.pv[lo, :], AluOpType.add).then_inc(sem.vps, 1)
     V.wait_ge(sem.vps, 4)
-    V.tensor_scalar(T.pos16[:, :], T.pw[:, :], low, None, AluOpType.add).then_inc(sem.vps, 1)
+    for hf in halves:
+        V.tensor_scalar(T.pos16[hf, :], T.pw[lo, :], low, None, AluOpType.add).then_inc(sem.vps, 1)
 
-    V.wait_ge(sem.vuh, 1)
-    S.wait_ge(sem.suh, 1)
-    S.wait_ge(sem.vnd, 2)
-    V.wait_ge(sem.vnd, 2)
-    V.wait_ge(sem.auc, len(far))
-    S.wait_ge(sem.aus, len(far))
-    a = me * BK
-    for i in range(2):
-        for q in (V, S):
-            q.wait_ge(sem["al%d" % i], list_count(mine[2 * i]) + list_count(mine[2 * i + 1]))
-        pick(T.sd, T.sds, 2 * i * BK, (2 * i + 2) * BK, T.uw, T.uws, 2 * UN, T.ll[:, 16 * i:16 * i + 16], "vsd%d" % i, "ssd%d" % i)
-        for vs, buf, lnd, relay, rsem, cast in (("vsd%d" % i, T.sd, T.land, T.rl, "rlc", u8), ("ssd%d" % i, T.sds, T.lands, T.rls, "rlp", same)):
-            g.wait_ge(sem[vs], 1)
-            if direct(core, order[i]):
-                fused([(far[m * h:m * h + h], cast(buf[:, (2 * i + m) * BK:(2 * i + m + 1) * BK]), d, cast(lnd[:, a:a + BK]), "ap%d" % me)
-                       for m, d in enumerate(pairs[order[i]])])
-            else:
-                fused([(hop(core, order[i]), cast(buf[:, 2 * i * BK:(2 * i + 2) * BK]), helper(core, order[i]), cast(relay[:, :]), rsem)])
-    pick(T.land, T.lands, a, a + BK, T.uw, T.uws, 2 * UN, T.lsx[:, me, :], "vown", "sown")
-    for q in (V, S):
-        q.wait_ge(sem.al2, list_count(mate))
-    off = T.rli[:, me, :] if blocked(mate) else T.ll[:, 32:40]
-    pick(T.sd, T.sds, 4 * BK, 5 * BK, T.uw, T.uws, 2 * UN, off, "vsd2", "ssd2")
-    for vs, buf, lnd, cast in (("vsd2", T.sd, T.land, u8), ("ssd2", T.sds, T.lands, same)):
-        g.wait_ge(sem[vs], 1)
-        fused([(near, cast(buf[:, 4 * BK:5 * BK]), mate, cast(lnd[:, a:a + BK]), "ap%d" % me)])
+    def due(d):
+        i, es = place(d, core)
+        return i + len(far) / len(es) + (1.5 if core in handed(d) else 0)
 
-    seq = [core, mate] + [d for d in mine[:4] if direct(d, p)] + [d for d in mine[:4] if not direct(d, p)]
+    seq = [core] + sorted([d for d in local if d != core], key=due)
     X.wait_ge(sem.vw, 1)
     for i, d in enumerate(seq):
         j = local.index(d)
         if d == core:
-            X.wait_ge(sem.vown, 1)
-            X.wait_ge(sem.sown, 1)
+            X.wait_ge(sem.vown, 2)
+            X.wait_ge(sem.sown, 2)
         else:
-            X.wait_ge(sem["ap%d" % j], 2 * len(near) if d == mate else 2 * h)
+            X.wait_ge(sem["ap%d" % j], 2 * len(far if core in handed(d) else place(d, core)[1]))
         b = j * BK
         X.matmul_mx(T.acc[:, 512 * i:512 * i + BK], T.qw[:, :], T.sw[:, :], T.land[:, b:b + BK], T.lands[:, b:b + BK], True, True).then_inc(sem["tm%d" % i], 1)
         q = (S, V)[i % 2]
@@ -271,11 +285,13 @@ def rank_program(g, core, T, topo):
     for q in (V, S):
         q.wait_ge(sem.evv, 3)
         q.wait_ge(sem.evs, 3)
-        q.wait_ge(sem.vps, 5)
-    V.tensor_copy(T.yo[:, 0:256], T.ys[:, :].indirect(T.pos16[:, 0:16])).then_inc(sem.gv, 1)
-    S.activation(T.yo[:, 256:512], T.ys[:, :].indirect(T.pos16[:, 16:32]), COPY).then_inc(sem.gs, 1)
-    g.sync.wait_ge(sem.gv, 1)
-    g.sync.wait_ge(sem.gs, 1)
-    g.sync.dma_start(T.y[:, :], T.yo[:, :]).then_inc(sem.st0, 16)
-    g.sync.wait_ge(sem.st0, 16)
+        q.wait_ge(sem.vps, 6)
+    for i, (c0, c1) in enumerate(((0, Y0), (Y0, W))):
+        m = (c0 + c1) // 2
+        V.tensor_copy(T.yo[:, c0:m], T.ys[:, :].indirect(T.pos16[:, c0 // 16:m // 16])).then_inc(sem.gv, 1)
+        S.activation(T.yo[:, m:c1], T.ys[:, :].indirect(T.pos16[:, m // 16:c1 // 16]), COPY).then_inc(sem.gs, 1)
+        Y.wait_ge(sem.gv, i + 1)
+        Y.wait_ge(sem.gs, i + 1)
+        Y.dma_start(T.y[:, c0:c1], T.yo[:, c0:c1]).then_inc(sem.st0, 16)
+    Y.wait_ge(sem.st0, 32)
     g.wait_ge(sem.sent, sent[0])

@@ -3,7 +3,8 @@ from concourse.mybir import dt, AluOpType, ActivationFunctionType
 
 UN, CR, W, CT = 160, 64, 512, 512
 BK = 2 * CR
-C0 = 352
+OWN, REM, ALL, WHOLE = (0, CR), (CR, BK), (0, BK), (0, UN)
+C0 = 336
 Y0 = 192
 COPY = ActivationFunctionType.Copy
 CODE, PLANE = "float8_e4m3fn_x4", "uint8"
@@ -18,16 +19,18 @@ SCRATCH = {
     "uo": ("sbuf", [128, UN], CODE), "uos": ("sbuf", [128, UN], PLANE),
     "uw": ("sbuf", [128, 2 * UN], CODE), "uws": ("sbuf", [128, 2 * UN], PLANE),
     "ll": ("sbuf", [128, 6, 8], "uint16"),
-    "rli": ("sbuf", [128, 2, 8], "uint16"),
+    "rli": ("sbuf", [128, 6, 8], "uint16"),
     "sd": ("sbuf", [128, 6 * BK], CODE), "sds": ("sbuf", [128, 6 * BK], PLANE),
-    "rl": ("sbuf", [128, 2 * BK], CODE), "rls": ("sbuf", [128, 2 * BK], PLANE),
+    "rl": ("sbuf", [128, 3 * BK], CODE), "rls": ("sbuf", [128, 3 * BK], PLANE),
+    "rw": ("sbuf", [128, UN], CODE), "rws": ("sbuf", [128, UN], PLANE),
+    "ux": ("sbuf", [128, UN], CODE), "uxs": ("sbuf", [128, UN], PLANE),
     "land": ("sbuf", [128, 6 * BK], CODE), "lands": ("sbuf", [128, 6 * BK], PLANE),
     "ys": ("sbuf", [128, 6 * BK], "float32"), "yo": ("sbuf", [128, W], "float32"),
     "acc": ("psum", [128, 512 * 6], "float32"),
 }
 SEMAPHORES = (["ldn", "ldu", "ldp", "ldw", "ldc0", "ldc1", "vnd", "vun", "vps", "vq", "vw", "vuo", "suo", "vuh", "suh",
-               "vown", "sown", "auc", "aus", "evv", "evs", "gv", "gs", "st0", "sent", "rla", "rc0", "rc1", "rp0", "rp1"]
-              + ["vsd%d" % i for i in range(3)] + ["ssd%d" % i for i in range(3)]
+               "vown", "sown", "auc", "aus", "evv", "evs", "gv", "gs", "st0", "sent", "rla", "ax0", "ax1", "vx", "sx"]
+              + ["r%d" % i for i in range(8)] + [s + str(i) for s in ("vsd", "ssd") for i in range(6)]
               + ["al%d" % i for i in range(6)] + ["ap%d" % i for i in range(6)] + ["tm%d" % i for i in range(6)])
 
 
@@ -46,6 +49,9 @@ def rank_program(g, core, T, topo):
     def blocked(c):
         return [d for d in others(c) if not topo.may_write(c, d)]
 
+    def apart(c, d):
+        return d in blocked(c) and c in blocked(d)
+
     def handed(c):
         if blocked(c):
             return blocked(c)
@@ -53,12 +59,20 @@ def rank_program(g, core, T, topo):
         return ([d for d in can if blocked(d)] + can)[:1]
 
     def helper(c, d):
-        to = handed(c)
-        can = [h for h in topo.cores_of(c) if h not in T.cores and topo.die(h) == topo.die(c) and all(topo.may_write(h, e) for e in to)]
-        return can[to.index(d) // 2]
+        def free(e):
+            return [h for h in topo.cores_of(e) if h not in T.cores and topo.die(h) == topo.die(e) and all(topo.may_write(h, r) for r in local)]
+        if len(blocked(c)) > 2:
+            return free(c)[blocked(c).index(d) // 2]
+        if blocked(c):
+            return free(c)[0]
+        return free(c)[0] if len(blocked(mate_of(c))) > 2 else free(mate_of(c))[1]
 
     def by_mate(c):
-        return [d for d in blocked(c) if c in blocked(d)]
+        return [d for d in blocked(c) if apart(c, d)]
+
+    def carrier(c, d, kind):
+        m = mate_of(c)
+        return helper(m, handed(m)[0]) if kind and apart(c, d) else helper(c, d)
 
     def late(c, d):
         return 0 if c not in handed(d) else 1 if c in by_mate(d) else 2
@@ -70,27 +84,36 @@ def rank_program(g, core, T, topo):
     def stages(c):
         far, near = on_off(c)
         via = sorted(handed(c), key=lambda d: late(c, d))
-        straight = sorted([d for d in others(c) if d not in via], key=lambda d: late(c, d))
+        straight = sorted([d for d in others(c) if d not in via], key=lambda d: (late(c, d), late(c, d) and len(blocked(d))))
+        m = mate_of(c)
+        first = [[(far, (straight or via[1:])[0], p), (near, via[0], p)] for p in (OWN, REM)]
         if len(via) == 1:
-            return [[(far, straight[0]), (near, via[0])], [(far[:4], straight[1]), (far[4:], straight[2]), (near, mate_of(c))]]
-        first = straight or via[0::2]
-        second = via if straight else via[1::2]
-        return [[(far, first[0]), (near, second[0])], [(far, first[1]), (near, second[1])], [(far + near, mate_of(c))]]
+            return first + [[(far, straight[1], ALL), (near, m, ALL)], [(far, straight[2], ALL)]]
+        if straight:
+            return first + [[(far + near, via[1], ALL)], [(far, straight[1], ALL), (near, m, ALL)]]
+        return [[(near[:4], via[2], WHOLE), (near[4:], via[3], WHOLE)], [(far[:4], via[1], OWN), (far[4:], via[0], OWN)], first[1],
+                [(far, via[2], REM), (near, via[3], REM)], [(far + near, m, ALL)]]
 
-    def served(c, h):
-        return [d for st in stages(c) for _, d in st if d in handed(c) and helper(c, d) == h]
+    def served(h):
+        return [(c, d) for c in local for d in handed(c) if h in (carrier(c, d, 0), carrier(c, d, 1))]
 
-    def place(c, d):
-        return [(i, es) for i, st in enumerate(stages(c)) for es, e in st if e == d][0]
+    def jobs_of(h):
+        return sorted([(i, kind, c, es, d, p) for c in local for i, st in enumerate(stages(c)) for es, d, p in st for kind in (0, 1)
+                       if d in handed(c) and carrier(c, d, kind and p != WHOLE) == h])
+
+    def parts(c, d):
+        return [(i, es) for i, st in enumerate(stages(c)) for es, e, p in st if e == d and p != WHOLE]
 
     def list_calls(c):
         far, near = on_off(c)
-        via = handed(c)
-        straight = [d for d in others(c) if d not in via]
-        on = near if straight else far + near
-        n = len(on) // len(via)
-        first = [(on[n * i:n * i + n], d) for i, d in enumerate(via)] + [(far[4 * i:4 * i + 4], d) for i, d in enumerate(straight[:2])]
-        return [first, [(far, d) for d in straight[2:]] + [(near, mate_of(c))]]
+        m, mu = mate_of(c), by_mate(c)
+        hl = [d for d in handed(c) if d not in mu]
+        st = sorted([d for d in others(c) if d not in handed(c)], key=lambda d: (c not in handed(d), parts(d, c)[0][0]))
+        if not blocked(c):
+            return [[(far[:4], st[0]), (far[4:], st[1])], [(near, hl[0])], [(far, st[2]), (near, m)]]
+        if st:
+            return [[(far[:4], st[0]), (far[4:], st[1])], [(near[4:], hl[0])], [(near[:4], mu[0]), (near[4:], m)]]
+        return [[(near[4:], m)], [(near[:4], mu[0])], [(far[:4], hl[0]), (far[4:], hl[1])]]
 
     def list_engines(c, d):
         return [es for call in list_calls(c) for es, e in call if e == d][0]
@@ -114,20 +137,22 @@ def rank_program(g, core, T, topo):
 
     rank = T.rank_of(core)
     if rank is None:
-        jobs = [c for c in local if any(helper(c, d) == core for d in handed(c))]
-        if not jobs:
+        to = served(core)
+        if not to:
             return
-        c, = jobs
-        to = served(c, core)
-        far = topo.engines(core, to[0])
-        j = local.index(c)
-        d, = [e for e in to if e not in by_mate(c)]
-        g.wait_ge(sem.rla, len(list_engines(c, d)))
-        fused([(far, T.rli[:, 0, :], d, T.ll[:, j, :], "al%d" % j)])
-        for i, d in enumerate(to):
-            for s, buf, lnd, cast in (("rc", T.rl, T.land, u8), ("rp", T.rls, T.lands, same)):
-                g.wait_ge(sem[s + str(i)], len(place(c, d)[1]))
-                fused([(far, cast(buf[:, i * BK:(i + 1) * BK]), d, cast(lnd[:, j * BK:(j + 1) * BK]), "ap%d" % j)])
+        far = topo.engines(core, to[0][1])
+        for c, d in [(c, d) for c in local for d in handed(c)]:
+            if d not in by_mate(c) and helper(c, d) == core:
+                g.wait_ge(sem.rla, len(list_engines(c, d)))
+                fused([(far[:4], T.rli[:, 0, :], d, T.ll[:, local.index(c), :], "al%d" % local.index(c))])
+        for i, (_, kind, c, es, d, (lo, hi)) in enumerate(jobs_of(core)):
+            j, k = local.index(c), to.index((c, d)) * BK
+            buf, lnd, cast = ((T.rl, T.land, u8), (T.rls, T.lands, same))[kind]
+            g.wait_ge(sem["r%d" % i], len(es))
+            if (lo, hi) == WHOLE:
+                fused([(far, cast((T.rw, T.rws)[kind][:, :]), d, cast((T.ux, T.uxs)[kind][:, :]), "ax%d" % kind)])
+            else:
+                fused([(far, cast(buf[:, k + lo:k + hi]), d, cast(lnd[:, j * BK + lo:j * BK + hi]), "ap%d" % j)])
         g.wait_ge(sem.sent, sent[0])
         return
 
@@ -159,7 +184,9 @@ def rank_program(g, core, T, topo):
         for es, d in call:
             src = T.lsx[:, local.index(d), :]
             if d in by_mate(core):
-                ts.append((es, src, mate, T.rli[:, by_mate(core).index(d), :], "rla"))
+                js = [local.index(e) for e in by_mate(core)]
+                run = slice(min(js), max(js) + 1)
+                ts.append((es, T.lsx[:, run, :], mate, T.rli[:, run, :], "rla"))
             elif d in handed(core):
                 ts.append((es, src, helper(core, d), T.rli[:, 0, :], "rla"))
             else:
@@ -167,7 +194,7 @@ def rank_program(g, core, T, topo):
         fused(ts)
 
     def wait_list(d):
-        n = (len(list_engines(d, core)), len(far) // max(1, len(by_mate(d))), len(far))[late(core, d)]
+        n = len(far) // len(by_mate(d)) if late(core, d) == 1 else len(far[:4] if late(core, d) else list_engines(d, core))
         for q in (V, S):
             q.wait_ge(sem["al%d" % local.index(d)], n)
 
@@ -196,11 +223,11 @@ def rank_program(g, core, T, topo):
     fused([(far, T.uos[:, :], partner, T.uws[:, UN:], "aus")])
     if by_mate(mate):
         n, j = len(far) // len(by_mate(mate)), local.index(mate)
-        g.wait_ge(sem.rla, sum(len(list_engines(mate, d)) for d in by_mate(mate)))
-        fused([(far[n * i:n * i + n], T.rli[:, i, :], d, T.ll[:, j, :], "al%d" % j) for i, d in enumerate(by_mate(mate))])
+        g.wait_ge(sem.rla, len(list_engines(mate, by_mate(mate)[0])))
+        fused([(far[n * i:n * i + n], T.rli[:, local.index(d), :], d, T.ll[:, j, :], "al%d" % j) for i, d in enumerate(by_mate(mate))])
 
     plan = stages(core)
-    count = [0] * 3
+    count = [0] * len(plan)
     V.wait_ge(sem.vuh, 1)
     S.wait_ge(sem.suh, 1)
     S.wait_ge(sem.vnd, 4)
@@ -208,7 +235,7 @@ def rank_program(g, core, T, topo):
     a = me * BK
     pick(T.land, T.lands, a, a + CR, T.uw, T.uws, UN, T.lsx[:, me, 0:4], "vown", "sown")
 
-    Y.wait_ge(sem.vown, 1)
+    Y.wait_ge(sem.vnd, 4)
     Y.dma_start(T.win[:, :], T.w[:, :]).then_inc(sem.ldw, 16)
     load(Y, T.pos32, T.pos, "ldp", range(0, 4))
 
@@ -217,31 +244,42 @@ def rank_program(g, core, T, topo):
         pick(T.sd, T.sds, j * BK + lo, j * BK + hi, T.uw, T.uws, UN if hi == CR else 2 * UN, T.ll[:, j, lo // 16:hi // 16], "vsd%d" % i, "ssd%d" % i)
         count[i] += 1
 
+    def send(i):
+        for k, vs, buf, lnd, relay, cast in ((0, "vsd%d" % i, T.sd, T.land, T.rl, u8), (1, "ssd%d" % i, T.sds, T.lands, T.rls, same)):
+            g.wait_ge(sem[vs], count[i])
+            ts = []
+            for es, d, (lo, hi) in plan[i]:
+                j = local.index(d)
+                src = cast(buf[:, j * BK + lo:j * BK + hi])
+                if d in handed(core):
+                    h = carrier(core, d, k)
+                    n = served(h).index((core, d)) * BK
+                    ts.append((es, src, h, cast(relay[:, n + lo:n + hi]), "r%d" % jobs_of(h).index((i, k, core, es, d, (lo, hi)))))
+                else:
+                    ts.append((es, src, d, cast(lnd[:, a + lo:a + hi]), "ap%d" % me))
+            fused(ts)
+
     for i, st in enumerate(plan):
-        for _, d in st:
-            if not late(core, d):
+        if st[0][2] == WHOLE:
+            for k, vs, buf, relay, cast in ((0, "vuh", T.uw, T.rw, u8), (1, "suh", T.uws, T.rws, same)):
+                g.wait_ge(sem[vs], 1)
+                fused([(es, cast(buf[:, 0:UN]), helper(core, d), cast(relay[:, :]), "r%d" % jobs_of(helper(core, d)).index((i, k, core, es, d, p)))
+                       for es, d, p in st])
+        for _, d, p in st:
+            if p == OWN:
                 wait_list(d)
                 part(i, d, 0, CR)
+        if all(p == OWN for _, _, p in st):
+            send(i)
     V.wait_ge(sem.auc, len(far))
     S.wait_ge(sem.aus, len(far))
     for i, st in enumerate(plan):
-        for _, d in sorted(st, key=lambda t: late(core, t[1])):
-            if late(core, d):
-                wait_list(d)
-            part(i, d, 0 if late(core, d) else CR, BK)
-        for k, vs, buf, lnd, relay, cast in (("rc", "vsd%d" % i, T.sd, T.land, T.rl, u8), ("rp", "ssd%d" % i, T.sds, T.lands, T.rls, same)):
-            g.wait_ge(sem[vs], count[i])
-            ts = []
-            for es, d in st:
-                j = local.index(d)
-                src = cast(buf[:, j * BK:(j + 1) * BK])
-                if d in handed(core):
-                    h = helper(core, d)
-                    n = served(core, h).index(d)
-                    ts.append((es, src, h, cast(relay[:, n * BK:(n + 1) * BK]), k + str(n)))
-                else:
-                    ts.append((es, src, d, cast(lnd[:, a:a + BK]), "ap%d" % me))
-            fused(ts)
+        if st[0][2] in (REM, ALL):
+            for _, d, p in sorted(st, key=lambda t: late(core, t[1])):
+                if p == ALL or late(core, d):
+                    wait_list(d)
+                part(i, d, *p)
+            send(i)
     pick(T.land, T.lands, a + CR, a + BK, T.uw, T.uws, 2 * UN, T.lsx[:, me, 4:8], "vown", "sown")
 
     V.wait_ge(sem.ldw, 16)
@@ -260,9 +298,17 @@ def rank_program(g, core, T, topo):
     for hf in halves:
         V.tensor_scalar(T.pos16[hf, :], T.pw[lo, :], low, None, AluOpType.add).then_inc(sem.vps, 1)
 
+    whole = [d for d in local if any(e == core and p == WHOLE for st in stages(d) for _, e, p in st)]
+    for d in whole:
+        j = local.index(d)
+        V.wait_ge(sem.ax0, len(far))
+        S.wait_ge(sem.ax1, len(far))
+        pick(T.land, T.lands, j * BK, j * BK + CR, T.ux, T.uxs, UN, T.lsx[:, j, 0:4], "vx", "sx")
+
     def due(d):
-        i, es = place(d, core)
-        return i + len(far) / len(es) + (1.5 if core in handed(d) else 0)
+        i = parts(d, core)[-1][0]
+        last = not blocked(d) and i == len(stages(d)) - 1
+        return (apart(core, d), last, core in handed(d), d != mate, i)
 
     seq = [core] + sorted([d for d in local if d != core], key=due)
     X.wait_ge(sem.vw, 1)
@@ -272,7 +318,10 @@ def rank_program(g, core, T, topo):
             X.wait_ge(sem.vown, 2)
             X.wait_ge(sem.sown, 2)
         else:
-            X.wait_ge(sem["ap%d" % j], 2 * len(far if core in handed(d) else place(d, core)[1]))
+            X.wait_ge(sem["ap%d" % j], sum(2 * len(far if core in handed(d) else es) for _, es in parts(d, core)))
+        if d in whole:
+            X.wait_ge(sem.vx, 1)
+            X.wait_ge(sem.sx, 1)
         b = j * BK
         X.matmul_mx(T.acc[:, 512 * i:512 * i + BK], T.qw[:, :], T.sw[:, :], T.land[:, b:b + BK], T.lands[:, b:b + BK], True, True).then_inc(sem["tm%d" % i], 1)
         q = (S, V)[i % 2]

from concourse.bass import DstId, RemoteDMATransfer
from concourse.mybir import dt, AluOpType, ActivationFunctionType

UN, CR, W, CT = 160, 64, 512, 512
BK = 2 * CR
OWN, REM, ALL, WHOLE = (0, CR), (CR, BK), (0, BK), (0, UN)
C0 = 336
Y0 = 192
COPY = ActivationFunctionType.Copy
CODE, PLANE = "float8_e4m3fn_x4", "uint8"
SCRATCH = {
    "cin": ("sbuf", [128, 4 * CT], "bfloat16"), "win": ("sbuf", [128, 512], "bfloat16"),
    "qc": ("sbuf", [128, CT], CODE), "sc": ("sbuf", [128, CT], PLANE),
    "qw": ("sbuf", [128, 128], CODE), "sw": ("sbuf", [128, 128], PLANE),
    "nd": ("sbuf", [128, 12, 4], "int32"), "lsx": ("sbuf", [128, 6, 8], "uint16"),
    "uni32": ("sbuf", [128, 20], "int32"), "uni16": ("sbuf", [128, 20], "uint16"),
    "pos32": ("sbuf", [128, 32], "int32"), "pt": ("sbuf", [128, 32], "int32"), "pu": ("sbuf", [128, 32], "int32"),
    "pv": ("sbuf", [128, 32], "int32"), "pw": ("sbuf", [128, 32], "int32"), "pos16": ("sbuf", [128, 32], "uint16"),
    "uo": ("sbuf", [128, UN], CODE), "uos": ("sbuf", [128, UN], PLANE),
    "uw": ("sbuf", [128, 2 * UN], CODE), "uws": ("sbuf", [128, 2 * UN], PLANE),
    "ll": ("sbuf", [128, 6, 8], "uint16"),
    "rli": ("sbuf", [128, 6, 8], "uint16"),
    "sd": ("sbuf", [128, 6 * BK], CODE), "sds": ("sbuf", [128, 6 * BK], PLANE),
    "rl": ("sbuf", [128, 3 * BK], CODE), "rls": ("sbuf", [128, 3 * BK], PLANE),
    "rw": ("sbuf", [128, UN], CODE), "rws": ("sbuf", [128, UN], PLANE),
    "ux": ("sbuf", [128, UN], CODE), "uxs": ("sbuf", [128, UN], PLANE),
    "land": ("sbuf", [128, 6 * BK], CODE), "lands": ("sbuf", [128, 6 * BK], PLANE),
    "ys": ("sbuf", [128, 6 * BK], "float32"), "yo": ("sbuf", [128, W], "float32"),
    "acc": ("psum", [128, 512 * 6], "float32"),
}
SEMAPHORES = (["ldn", "ldu", "ldp", "ldw", "ldc0", "ldc1", "vnd", "vun", "vps", "vq", "vw", "vuo", "suo", "vuh", "suh",
               "vown", "sown", "auc", "aus", "evv", "evs", "gv", "gs", "st0", "sent", "rla", "ax0", "ax1", "vx", "sx"]
              + ["r%d" % i for i in range(8)] + [s + str(i) for s in ("vsd", "ssd") for i in range(6)]
              + ["al%d" % i for i in range(6)] + ["ap%d" % i for i in range(6)] + ["tm%d" % i for i in range(6)])


def rank_program(g, core, T, topo):
    sem = T.sem
    local = [c for c in T.cores if topo.host(c) == topo.host(core)]
    away = [c for c in T.cores if c not in local]

    def mate_of(c):
        return [d for d in local if d != c and d in topo.cores_of(c)][0]

    def others(c):
        n = local.index(c)
        return [d for d in local[n + 1:] + local[:n] if d != mate_of(c)]

    def blocked(c):
        return [d for d in others(c) if not topo.may_write(c, d)]

    def apart(c, d):
        return d in blocked(c) and c in blocked(d)

    def handed(c):
        if blocked(c):
            return blocked(c)
        can = [d for d in others(c) if topo.may_write(d, c)]
        return ([d for d in can if blocked(d)] + can)[:1]

    def helper(c, d):
        def free(e):
            return [h for h in topo.cores_of(e) if h not in T.cores and topo.die(h) == topo.die(e) and all(topo.may_write(h, r) for r in local)]
        if len(blocked(c)) > 2:
            return free(c)[blocked(c).index(d) // 2]
        if blocked(c):
            return free(c)[0]
        return free(c)[0] if len(blocked(mate_of(c))) > 2 else free(mate_of(c))[1]

    def by_mate(c):
        return [d for d in blocked(c) if apart(c, d)]

    def carrier(c, d, kind):
        m = mate_of(c)
        return helper(m, handed(m)[0]) if kind and apart(c, d) else helper(c, d)

    def late(c, d):
        return 0 if c not in handed(d) else 1 if c in by_mate(d) else 2

    def on_off(c):
        off = topo.engines(c, [d for d in T.cores if topo.host(d) != topo.host(c) and topo.may_write(c, d)][0])
        return off, [e for e in topo.engines(c, mate_of(c)) if e not in off]

    def stages(c):
        far, near = on_off(c)
        via = sorted(handed(c), key=lambda d: late(c, d))
        straight = sorted([d for d in others(c) if d not in via], key=lambda d: (late(c, d), late(c, d) and len(blocked(d))))
        m = mate_of(c)
        first = [[(far, (straight or via[1:])[0], p), (near, via[0], p)] for p in (OWN, REM)]
        if len(via) == 1:
            return first + [[(far, straight[1], ALL), (near, m, ALL)], [(far, straight[2], ALL)]]
        if straight:
            return first + [[(far + near, via[1], ALL)], [(far, straight[1], ALL), (near, m, ALL)]]
        return [[(near[:4], via[2], WHOLE), (near[4:], via[3], WHOLE)], [(far[:4], via[1], OWN), (far[4:], via[0], OWN)], first[1],
                [(far, via[2], REM), (near, via[3], REM)], [(far + near, m, ALL)]]

    def served(h):
        return [(c, d) for c in local for d in handed(c) if h in (carrier(c, d, 0), carrier(c, d, 1))]

    def jobs_of(h):
        return sorted([(i, kind, c, es, d, p) for c in local for i, st in enumerate(stages(c)) for es, d, p in st for kind in (0, 1)
                       if d in handed(c) and carrier(c, d, kind and p != WHOLE) == h])

    def parts(c, d):
        return [(i, es) for i, st in enumerate(stages(c)) for es, e, p in st if e == d and p != WHOLE]

    def list_calls(c):
        far, near = on_off(c)
        m, mu = mate_of(c), by_mate(c)
        hl = [d for d in handed(c) if d not in mu]
        st = sorted([d for d in others(c) if d not in handed(c)], key=lambda d: (c not in handed(d), parts(d, c)[0][0]))
        if not blocked(c):
            return [[(far[:4], st[0]), (far[4:], st[1])], [(near, hl[0])], [(far, st[2]), (near, m)]]
        if st:
            return [[(far[:4], st[0]), (far[4:], st[1])], [(near[4:], hl[0])], [(near[:4], mu[0]), (near[4:], m)]]
        return [[(near[4:], m)], [(near[:4], mu[0])], [(far[:4], hl[0]), (far[4:], hl[1])]]

    def list_engines(c, d):
        return [es for call in list_calls(c) for es, e in call if e == d][0]

    sent = [0]

    def fused(transfers):
        ts = []
        for es, src, d, view, s in transfers:
            rid, pid = topo.addr(d, core)
            ts.append(RemoteDMATransfer(dst_ids=[DstId(rid=rid, pnc=pid)], dma_engine_mask=sum(1 << e for e in es), remote_sem=sem[s],
                                        srcs=[src], dsts=[view], alu_op=0))
            sent[0] += len(es)
        g.remote_dma_fused(ts, local_sem=sem.sent)

    def u8(v):
        return v.bitcast(dt.uint8)

    def same(v):
        return v

    rank = T.rank_of(core)
    if rank is None:
        to = served(core)
        if not to:
            return
        far = topo.engines(core, to[0][1])
        for c, d in [(c, d) for c in local for d in handed(c)]:
            if d not in by_mate(c) and helper(c, d) == core:
                g.wait_ge(sem.rla, len(list_engines(c, d)))
                fused([(far[:4], T.rli[:, 0, :], d, T.ll[:, local.index(c), :], "al%d" % local.index(c))])
        for i, (_, kind, c, es, d, (lo, hi)) in enumerate(jobs_of(core)):
            j, k = local.index(c), to.index((c, d)) * BK
            buf, lnd, cast = ((T.rl, T.land, u8), (T.rls, T.lands, same))[kind]
            g.wait_ge(sem["r%d" % i], len(es))
            if (lo, hi) == WHOLE:
                fused([(far, cast((T.rw, T.rws)[kind][:, :]), d, cast((T.ux, T.uxs)[kind][:, :]), "ax%d" % kind)])
            else:
                fused([(far, cast(buf[:, k + lo:k + hi]), d, cast(lnd[:, j * BK + lo:j * BK + hi]), "ap%d" % j)])
        g.wait_ge(sem.sent, sent[0])
        return

    mate = mate_of(core)
    me = local.index(core)
    partner = away[me]
    far, near = on_off(core)
    hb, ab = T.rank_of(local[0]), T.rank_of(away[0])
    V, S, X, Y = g.vector, g.scalar, g.tensor, g.sync
    halves = (slice(0, 64), slice(64, 128))

    def load(q, buf, src, s, groups):
        for i in groups:
            q.dma_start(buf[16 * i:16 * i + 16], src[:, :]).then_inc(sem[s], 16)

    load(Y, T.nd, T.need, "ldn", range(0, 2))
    load(S, T.nd, T.need, "ldn", range(2, 4))
    S.dma_start(T.cin[:, 0:4 * C0], T.c[:, 0:4 * C0]).then_inc(sem.ldc0, 16)
    load(Y, T.uni32, T.uni, "ldu", range(0, 4))
    Y.dma_start(T.cin[:, 4 * C0:], T.c[:, 4 * C0:]).then_inc(sem.ldc1, 16)

    V.wait_ge(sem.ldn, 64)
    for hf in halves:
        V.tensor_copy(T.lsx[hf, :, 0:4], T.nd[0:64, hb:hb + 6, :]).then_inc(sem.vnd, 1)
        V.tensor_scalar(T.lsx[hf, :, 4:8], T.nd[0:64, ab:ab + 6, :], UN, None, AluOpType.add).then_inc(sem.vnd, 1)
    g.wait_ge(sem.vnd, 4)
    for call in list_calls(core):
        ts = []
        for es, d in call:
            src = T.lsx[:, local.index(d), :]
            if d in by_mate(core):
                js = [local.index(e) for e in by_mate(core)]
                run = slice(min(js), max(js) + 1)
                ts.append((es, T.lsx[:, run, :], mate, T.rli[:, run, :], "rla"))
            elif d in handed(core):
                ts.append((es, src, helper(core, d), T.rli[:, 0, :], "rla"))
            else:
                ts.append((es, src, d, T.ll[:, me, :], "al%d" % me))
        fused(ts)

    def wait_list(d):
        n = len(far) // len(by_mate(d)) if late(core, d) == 1 else len(far[:4] if late(core, d) else list_engines(d, core))
        for q in (V, S):
            q.wait_ge(sem["al%d" % local.index(d)], n)

    V.wait_ge(sem.ldc0, 16)
    V.quantize_mx(T.qc[:, 0:C0], T.sc[:, 0:C0], T.cin[:, 0:4 * C0]).then_inc(sem.vq, 1)
    V.wait_ge(sem.ldu, 64)
    for hf in halves:
        V.tensor_copy(T.uni16[hf, :], T.uni32[0:64, :]).then_inc(sem.vun, 1)
    V.wait_ge(sem.ldc1, 16)
    V.quantize_mx(T.qc[:, C0:], T.sc[:, C0:], T.cin[:, 4 * C0:]).then_inc(sem.vq, 1)

    def pick(codes, planes, c0, c1, wc, wp, n, off, vs, ss):
        V.tensor_copy(codes[:, c0:c1].bitcast(dt.uint32), wc[:, 0:n].bitcast(dt.uint32).indirect(off)).then_inc(sem[vs], 1)
        S.activation(planes[:, c0:c1], wp[:, 0:n].indirect(off), COPY).then_inc(sem[ss], 1)

    for q in (V, S):
        q.wait_ge(sem.vun, 2)
        q.wait_ge(sem.vq, 2)
    host = topo.host(core)
    o10, h10 = 10 * (1 - host), 10 * host
    pick(T.uo, T.uos, 0, UN, T.qc, T.sc, CT, T.uni16[:, o10:o10 + 10], "vuo", "suo")
    pick(T.uw, T.uws, 0, UN, T.qc, T.sc, CT, T.uni16[:, h10:h10 + 10], "vuh", "suh")
    g.wait_ge(sem.vuo, 1)
    fused([(far, u8(T.uo[:, :]), partner, u8(T.uw[:, UN:]), "auc")])
    g.wait_ge(sem.suo, 1)
    fused([(far, T.uos[:, :], partner, T.uws[:, UN:], "aus")])
    if by_mate(mate):
        n, j = len(far) // len(by_mate(mate)), local.index(mate)
        g.wait_ge(sem.rla, len(list_engines(mate, by_mate(mate)[0])))
        fused([(far[n * i:n * i + n], T.rli[:, local.index(d), :], d, T.ll[:, j, :], "al%d" % j) for i, d in enumerate(by_mate(mate))])

    plan = stages(core)
    count = [0] * len(plan)
    V.wait_ge(sem.vuh, 1)
    S.wait_ge(sem.suh, 1)
    S.wait_ge(sem.vnd, 4)
    V.wait_ge(sem.vnd, 4)
    a = me * BK
    pick(T.land, T.lands, a, a + CR, T.uw, T.uws, UN, T.lsx[:, me, 0:4], "vown", "sown")

    Y.wait_ge(sem.vnd, 4)
    Y.dma_start(T.win[:, :], T.w[:, :]).then_inc(sem.ldw, 16)
    load(Y, T.pos32, T.pos, "ldp", range(0, 4))

    def part(i, d, lo, hi):
        j = local.index(d)
        pick(T.sd, T.sds, j * BK + lo, j * BK + hi, T.uw, T.uws, UN if hi == CR else 2 * UN, T.ll[:, j, lo // 16:hi // 16], "vsd%d" % i, "ssd%d" % i)
        count[i] += 1

    def send(i):
        for k, vs, buf, lnd, relay, cast in ((0, "vsd%d" % i, T.sd, T.land, T.rl, u8), (1, "ssd%d" % i, T.sds, T.lands, T.rls, same)):
            g.wait_ge(sem[vs], count[i])
            ts = []
            for es, d, (lo, hi) in plan[i]:
                j = local.index(d)
                src = cast(buf[:, j * BK + lo:j * BK + hi])
                if d in handed(core):
                    h = carrier(core, d, k)
                    n = served(h).index((core, d)) * BK
                    ts.append((es, src, h, cast(relay[:, n + lo:n + hi]), "r%d" % jobs_of(h).index((i, k, core, es, d, (lo, hi)))))
                else:
                    ts.append((es, src, d, cast(lnd[:, a + lo:a + hi]), "ap%d" % me))
            fused(ts)

    for i, st in enumerate(plan):
        if st[0][2] == WHOLE:
            for k, vs, buf, relay, cast in ((0, "vuh", T.uw, T.rw, u8), (1, "suh", T.uws, T.rws, same)):
                g.wait_ge(sem[vs], 1)
                fused([(es, cast(buf[:, 0:UN]), helper(core, d), cast(relay[:, :]), "r%d" % jobs_of(helper(core, d)).index((i, k, core, es, d, p)))
                       for es, d, p in st])
        for _, d, p in st:
            if p == OWN:
                wait_list(d)
                part(i, d, 0, CR)
        if all(p == OWN for _, _, p in st):
            send(i)
    V.wait_ge(sem.auc, len(far))
    S.wait_ge(sem.aus, len(far))
    for i, st in enumerate(plan):
        if st[0][2] in (REM, ALL):
            for _, d, p in sorted(st, key=lambda t: late(core, t[1])):
                if p == ALL or late(core, d):
                    wait_list(d)
                part(i, d, *p)
            send(i)
    pick(T.land, T.lands, a + CR, a + BK, T.uw, T.uws, 2 * UN, T.lsx[:, me, 4:8], "vown", "sown")

    V.wait_ge(sem.ldw, 16)
    V.quantize_mx(T.qw[:, :], T.sw[:, :], T.win[:, :]).then_inc(sem.vw, 1)
    own_c, away_c = -BK * hb, CR - BK * ab
    low, high = (own_c, away_c) if hb < ab else (away_c, own_c)
    lo = halves[0]
    V.wait_ge(sem.ldp, 64)
    V.tensor_scalar(T.pt[lo, :], T.pos32[lo, :], -CR, None, AluOpType.bitwise_and).then_inc(sem.vps, 1)
    V.wait_ge(sem.vps, 1)
    V.tensor_tensor(T.pu[lo, :], T.pos32[lo, :], T.pt[lo, :], AluOpType.add).then_inc(sem.vps, 1)
    V.tensor_scalar(T.pv[lo, :], T.pt[lo, :], 6 * CR, high - low, AluOpType.is_ge, AluOpType.mult).then_inc(sem.vps, 1)
    V.wait_ge(sem.vps, 3)
    V.tensor_tensor(T.pw[lo, :], T.pu[lo, :], T.pv[lo, :], AluOpType.add).then_inc(sem.vps, 1)
    V.wait_ge(sem.vps, 4)
    for hf in halves:
        V.tensor_scalar(T.pos16[hf, :], T.pw[lo, :], low, None, AluOpType.add).then_inc(sem.vps, 1)

    whole = [d for d in local if any(e == core and p == WHOLE for st in stages(d) for _, e, p in st)]
    for d in whole:
        j = local.index(d)
        V.wait_ge(sem.ax0, len(far))
        S.wait_ge(sem.ax1, len(far))
        pick(T.land, T.lands, j * BK, j * BK + CR, T.ux, T.uxs, UN, T.lsx[:, j, 0:4], "vx", "sx")

    def due(d):
        i = parts(d, core)[-1][0]
        last = not blocked(d) and i == len(stages(d)) - 1
        return (apart(core, d), last, core in handed(d), d != mate, i)

    seq = [core] + sorted([d for d in local if d != core], key=due)
    X.wait_ge(sem.vw, 1)
    for i, d in enumerate(seq):
        j = local.index(d)
        if d == core:
            X.wait_ge(sem.vown, 2)
            X.wait_ge(sem.sown, 2)
        else:
            X.wait_ge(sem["ap%d" % j], sum(2 * len(far if core in handed(d) else es) for _, es in parts(d, core)))
        if d in whole:
            X.wait_ge(sem.vx, 1)
            X.wait_ge(sem.sx, 1)
        b = j * BK
        X.matmul_mx(T.acc[:, 512 * i:512 * i + BK], T.qw[:, :], T.sw[:, :], T.land[:, b:b + BK], T.lands[:, b:b + BK], True, True).then_inc(sem["tm%d" % i], 1)
        q = (S, V)[i % 2]
        q.wait_ge(sem["tm%d" % i], 1)
        if i % 2:
            V.tensor_copy(T.ys[:, b:b + BK], T.acc[:, 512 * i:512 * i + BK]).then_inc(sem.evv, 1)
        else:
            S.activation(T.ys[:, b:b + BK], T.acc[:, 512 * i:512 * i + BK], COPY).then_inc(sem.evs, 1)

    for q in (V, S):
        q.wait_ge(sem.evv, 3)
        q.wait_ge(sem.evs, 3)
        q.wait_ge(sem.vps, 6)
    for i, (c0, c1) in enumerate(((0, Y0), (Y0, W))):
        m = (c0 + c1) // 2
        V.tensor_copy(T.yo[:, c0:m], T.ys[:, :].indirect(T.pos16[:, c0 // 16:m // 16])).then_inc(sem.gv, 1)
        S.activation(T.yo[:, m:c1], T.ys[:, :].indirect(T.pos16[:, m // 16:c1 // 16]), COPY).then_inc(sem.gs, 1)
        Y.wait_ge(sem.gv, i + 1)
        Y.wait_ge(sem.gs, i + 1)
        Y.dma_start(T.y[:, c0:c1], T.yo[:, c0:c1]).then_inc(sem.st0, 16)
    Y.wait_ge(sem.st0, 32)
    g.wait_ge(sem.sent, sent[0])
